import numpy as np
import ml_dtypes

BF16 = ml_dtypes.bfloat16


def bf(x):
    return np.asarray(x, np.float32).astype(BF16)


def f32(x):
    return np.asarray(x, np.float32)


def f64(x):
    return np.asarray(x).astype(np.float64)


def striped(idx):
    return np.tile(idx.reshape(-1, 16).T, (8, 1))


def rows(idx, k):
    return np.tile(idx, (k, 1))


def look(tab, idx):
    return np.take_along_axis(f64(tab), rows(idx, len(tab)), axis=1)


K, S, V, N = 256, 2048, 512, 512


def setup_inputs():
    return {"tab": f32(np.random.standard_normal((2, K, S))), "offs": striped(np.random.permutation(S)[:N])}


def reference(tab, offs):
    idx = offs[:16].T.reshape(-1)
    x = (look(tab[0], idx) >= 0.25) * 0.5 * np.tanh(look(tab[1], idx))
    return x

@@ -1,0 +1,46 @@
+import concourse.mybir as mybir
+
+F32, U16 = mybir.dt.float32, mybir.dt.uint16
+ALU = mybir.AluOpType
+TANH = mybir.ActivationFunctionType.Tanh
+
+P = 128
+THRESHOLD = 0.25
+GAIN = 0.5
+
+
+def tile_lookup_steptanh_out_kernel(tc, tab, offs, out):
+    nc = tc.nc
+    places = tab.shape[2]
+    n = out.shape[1]
+    blocks = tab.shape[1] // P
+
+    with (
+        tc.tile_pool(name="list", bufs=1) as list_pool,
+        tc.tile_pool(name="tables", bufs=blocks) as tables,
+        tc.tile_pool(name="work", bufs=blocks) as work,
+    ):
+        offsets = list_pool.tile([P, offs.shape[1]], U16, name="offsets")
+        nc.sync.dma_start(offsets[:], offs)
+
+        values, keys = [], []
+        for b in range(blocks):
+            rows = slice(b * P, (b + 1) * P)
+            value_tile = tables.tile([P, places], F32, name="value_tile")
+            nc.sync.dma_start(value_tile[:], tab[1, rows, :])
+            key_tile = tables.tile([P, places], F32, name="key_tile")
+            nc.sync.dma_start(key_tile[:], tab[0, rows, :])
+            values.append(value_tile)
+            keys.append(key_tile)
+
+        for b in range(blocks):
+            rows = slice(b * P, (b + 1) * P)
+            squashed = work.tile([P, n], F32, name="squashed")
+            nc.scalar.activation(squashed[:], values[b][:].indirect(offsets[:]), TANH)
+            step = work.tile([P, n], F32, name="step")
+            nc.vector.tensor_scalar(
+                step[:], keys[b][:].indirect(offsets[:]), THRESHOLD, GAIN, op0=ALU.is_ge, op1=ALU.mult
+            )
+            x = work.tile([P, n], F32, name="x")
+            nc.vector.tensor_tensor(x[:], step[:], squashed[:], op=ALU.mult)
+            nc.sync.dma_start(out[rows, :], x[:])

@@ -7,6 +7,7 @@ TANH = mybir.ActivationFunctionType.Tanh
 P = 128
 THRESHOLD = 0.25
 GAIN = 0.5
+PIECES = 2
 
 
 def tile_lookup_steptanh_out_kernel(tc, tab, offs, out):
@@ -18,7 +19,7 @@ def tile_lookup_steptanh_out_kernel(tc, tab, offs, out):
     with (
         tc.tile_pool(name="list", bufs=1) as list_pool,
         tc.tile_pool(name="tables", bufs=blocks) as tables,
-        tc.tile_pool(name="work", bufs=blocks) as work,
+        tc.tile_pool(name="work", bufs=PIECES * blocks) as work,
     ):
         offsets = list_pool.tile([P, offs.shape[1]], U16, name="offsets")
         nc.sync.dma_start(offsets[:], offs)
@@ -33,14 +34,18 @@ def tile_lookup_steptanh_out_kernel(tc, tab, offs, out):
             values.append(value_tile)
             keys.append(key_tile)
 
+        width = n // PIECES
         for b in range(blocks):
             rows = slice(b * P, (b + 1) * P)
-            squashed = work.tile([P, n], F32, name="squashed")
-            nc.scalar.activation(squashed[:], values[b][:].indirect(offsets[:]), TANH)
-            step = work.tile([P, n], F32, name="step")
-            nc.vector.tensor_scalar(
-                step[:], keys[b][:].indirect(offsets[:]), THRESHOLD, GAIN, op0=ALU.is_ge, op1=ALU.mult
-            )
-            x = work.tile([P, n], F32, name="x")
-            nc.vector.tensor_tensor(x[:], step[:], squashed[:], op=ALU.mult)
-            nc.sync.dma_start(out[rows, :], x[:])
+            for piece in range(PIECES):
+                columns = slice(piece * width, (piece + 1) * width)
+                entries = offsets[:, piece * width // 16 : (piece + 1) * width // 16]
+                squashed = work.tile([P, width], F32, name="squashed")
+                nc.scalar.activation(squashed[:], values[b][:].indirect(entries), TANH)
+                step = work.tile([P, width], F32, name="step")
+                nc.vector.tensor_scalar(
+                    step[:], keys[b][:].indirect(entries), THRESHOLD, GAIN, op0=ALU.is_ge, op1=ALU.mult
+                )
+                x = work.tile([P, width], F32, name="x")
+                nc.vector.tensor_tensor(x[:], step[:], squashed[:], op=ALU.mult)
+                nc.sync.dma_start(out[rows, columns], x[:])

@@ -27,10 +27,10 @@ def tile_lookup_steptanh_out_kernel(tc, tab, offs, out):
         values, keys = [], []
         for b in range(blocks):
             rows = slice(b * P, (b + 1) * P)
-            value_tile = tables.tile([P, places], F32, name="value_tile")
-            nc.sync.dma_start(value_tile[:], tab[1, rows, :])
             key_tile = tables.tile([P, places], F32, name="key_tile")
             nc.sync.dma_start(key_tile[:], tab[0, rows, :])
+            value_tile = tables.tile([P, places], F32, name="value_tile")
+            nc.sync.dma_start(value_tile[:], tab[1, rows, :])
             values.append(value_tile)
             keys.append(key_tile)
 

import concourse.mybir as mybir

F32, U16 = mybir.dt.float32, mybir.dt.uint16
ALU = mybir.AluOpType
TANH = mybir.ActivationFunctionType.Tanh

P = 128
THRESHOLD = 0.25
GAIN = 0.5
PIECES = 2


def tile_lookup_steptanh_out_kernel(tc, tab, offs, out):
    nc = tc.nc
    places = tab.shape[2]
    n = out.shape[1]
    blocks = tab.shape[1] // P

    with (
        tc.tile_pool(name="list", bufs=1) as list_pool,
        tc.tile_pool(name="tables", bufs=blocks) as tables,
        tc.tile_pool(name="work", bufs=PIECES * blocks) as work,
    ):
        offsets = list_pool.tile([P, offs.shape[1]], U16, name="offsets")
        nc.sync.dma_start(offsets[:], offs)

        values, keys = [], []
        for b in range(blocks):
            rows = slice(b * P, (b + 1) * P)
            key_tile = tables.tile([P, places], F32, name="key_tile")
            nc.sync.dma_start(key_tile[:], tab[0, rows, :])
            value_tile = tables.tile([P, places], F32, name="value_tile")
            nc.sync.dma_start(value_tile[:], tab[1, rows, :])
            values.append(value_tile)
            keys.append(key_tile)

        width = n // PIECES
        for b in range(blocks):
            rows = slice(b * P, (b + 1) * P)
            for piece in range(PIECES):
                columns = slice(piece * width, (piece + 1) * width)
                entries = offsets[:, piece * width // 16 : (piece + 1) * width // 16]
                squashed = work.tile([P, width], F32, name="squashed")
                nc.scalar.activation(squashed[:], values[b][:].indirect(entries), TANH)
                step = work.tile([P, width], F32, name="step")
                nc.vector.tensor_scalar(
                    step[:], keys[b][:].indirect(entries), THRESHOLD, GAIN, op0=ALU.is_ge, op1=ALU.mult
                )
                x = work.tile([P, width], F32, name="x")
                nc.vector.tensor_tensor(x[:], step[:], squashed[:], op=ALU.mult)
                nc.sync.dma_start(out[rows, columns], x[:])
